import numpy as np
import ml_dtypes


def mxq(x, axis, fmt="e4m3"):
    dtype, down = {"e4m3": (ml_dtypes.float8_e4m3fn, 7), "e5m2": (ml_dtypes.float8_e5m2, 14)}[fmt]
    v = np.moveaxis(np.asarray(x, np.float32).astype(ml_dtypes.bfloat16).astype(np.float64), axis, -1)
    blocks = v.reshape(v.shape[:-1] + (-1, 32))
    amax = np.abs(blocks).max(-1, keepdims=True)
    byte = np.maximum(np.where(amax > 0, np.frexp(amax)[1] - 1 + 127, 0) - down, 1)
    scale = np.exp2(byte - 127.0)
    codes = (blocks / scale).astype(np.float32).astype(dtype).astype(np.float64)
    return np.moveaxis((codes * scale).reshape(v.shape), -1, axis)


WIDE = False


def mx_kscale(k):
    if not WIDE:
        return np.ones(k)
    levels = np.array([10, -10, 5, -5, 0])
    if k % 512:
        return np.exp2(np.random.permutation(np.resize(levels, k // 32))).repeat(32)
    a = np.empty((k // 512, 16))
    for p in range(k // 512):
        a[p, :8] = np.random.permutation(np.resize(levels, 8))
        for g in range(8):
            far = levels[np.abs(levels - a[p, g]) >= 10]
            a[p, g + 8] = far[np.random.randint(len(far))]
    return np.exp2(a.ravel()).repeat(32)


def f64(x):
    return np.asarray(x).astype(np.float64)


def striped(idx):
    return np.tile(idx.reshape(-1, 16).T, (8, 1)).astype(np.uint16)


def unstriped(offs):
    return offs[:16].T.reshape(-1).astype(np.int64)


def pack_weight(w):
    k, n = w.shape
    w = f64(np.asarray(w, np.float32).astype(ml_dtypes.bfloat16)).reshape(k // 32, 32, n)
    amax = np.abs(w).max(1)
    byte = np.clip(np.where(amax > 0, np.frexp(amax)[1] - 1 + 127 - 7, 1), 1, 254)
    scaled = (w * np.exp2(127.0 - byte)[:, None, :]).reshape(k, n).astype(np.float32)
    words = np.ascontiguousarray(scaled.reshape(k // 512, 128, 4, n).transpose(0, 1, 3, 2)).astype(ml_dtypes.float8_e4m3fn).view(np.uint8)
    return words, np.ascontiguousarray(byte.astype(np.uint8).reshape(k // 512, 16, n))


def unpack_weight(words, scales):
    g, p, n, _ = words.shape
    vals = np.ascontiguousarray(words).view(ml_dtypes.float8_e4m3fn).astype(np.float64) * np.repeat(np.exp2(scales.astype(np.float64) - 127.0), 8, axis=1)[..., None]
    return vals.transpose(0, 1, 3, 2).reshape(g * 512, n)


E2M1 = np.array([0.0, 0.5, 1.0, 1.5, 2.0, 3.0, 4.0, 6.0, -0.0, -0.5, -1.0, -1.5, -2.0, -3.0, -4.0, -6.0])


def pack_fp4(w):
    k, n = w.shape
    w = f64(np.asarray(w, np.float32).astype(ml_dtypes.bfloat16)).reshape(k // 32, 32, n)
    amax = np.abs(w).max(1)
    mant, ex = np.frexp(amax / 6.0)
    byte = np.clip(np.where(amax > 0, np.where(mant > 0.5, ex, ex - 1) + 127, 1), 1, 254)
    scaled = (w * np.exp2(127.0 - byte)[:, None, :]).reshape(k, n).astype(np.float32)
    c = np.ascontiguousarray(scaled.reshape(k // 512, 128, 4, n).transpose(0, 1, 3, 2)).astype(ml_dtypes.float4_e2m1fn).view(np.uint8) & 0xF
    words = (c[..., 0::2] | (c[..., 1::2] << 4)).reshape(k // 512, 128, 2 * n)
    return np.ascontiguousarray(words), np.ascontiguousarray(byte.astype(np.uint8).reshape(k // 512, 16, n))


def unpack_fp4(words, scales):
    g, _, n = scales.shape
    words = np.ascontiguousarray(words).reshape(g, 128, n, 2)
    nib = np.empty((g, 128, n, 4), np.uint8)
    nib[..., 0::2] = words & 0xF
    nib[..., 1::2] = words >> 4
    vals = E2M1[nib] * np.repeat(np.exp2(scales.astype(np.float64) - 127.0), 8, axis=1)[..., None]
    return vals.transpose(0, 1, 3, 2).reshape(g * 512, n)


K, T, S, D, H, N = 512, 2048, 1024, 3, 512, 256


def setup_inputs():
    n = np.random.standard_normal
    s = mx_kscale(K)[:, None]
    u = mx_kscale(H)
    packed_xT = pack_weight(n((K, T)) * s)
    packed_w2 = pack_fp4(n((H, N)) / np.sqrt(H) / u[:, None])
    return {
        "x_words": packed_xT[0],
        "x_scales": packed_xT[1],
        "w1": (n((K, H)) / np.sqrt(K) / s * u).astype(np.float32),
        "w2_words": packed_w2[0],
        "w2_scales": packed_w2[1],
        "taps": (n((H, D)) / np.sqrt(D)).astype(np.float32),
        "offs": striped(np.random.permutation(T)[:S]),
    }


def reference(x_words, x_scales, w1, w2_words, w2_scales, taps, offs):
    xq = unpack_weight(x_words, x_scales)[:, unstriped(offs)]
    h = mxq(f64(w1), 0, "e4m3").T @ xq
    z = f64(taps)[:, 0:1] * h + f64(taps)[:, 1:2] * (np.pad(h, ((0, 0), (1, 0)))[:, :S]) + f64(taps)[:, 2:3] * (np.pad(h, ((0, 0), (2, 0)))[:, :S])
    return unpack_fp4(w2_words, w2_scales).T @ mxq(z, 0, "e4m3")

@@ -1,0 +1,192 @@
+from contextlib import ExitStack
+
+import concourse.mybir as mybir
+
+F32 = mybir.dt.float32
+BF16 = mybir.dt.bfloat16
+I32 = mybir.dt.int32
+U32 = mybir.dt.uint32
+U16 = mybir.dt.uint16
+U8 = mybir.dt.uint8
+FP8X4 = mybir.dt.float8_e4m3fn_x4
+FP4X4 = mybir.dt.float4_e2m1fn_x4
+MULT = mybir.AluOpType.mult
+ADD = mybir.AluOpType.add
+COPY = mybir.ActivationFunctionType.Copy
+
+K, T, S, D, H, N = 512, 2048, 1024, 3, 512, 256
+P = 128
+PACK = 4
+BANK = 512
+PAD = 8
+FLOPS = 2 * K * H * S + 2 * H * N * S
+
+CHUNKS = [(256,"SV",2),(256,"SV",2),(256,"SV",2),(256,"SV",2)]
+WORD_GATHERS = [256,256,512]
+BYTE_GATHERS = [1024]
+W1_SPLIT = 80
+G_COLS = 64
+H_BANKS = 6
+O_BANKS = 2
+
+
+def tile_picked_dconv_none_p_kernel(tc, x_words, x_scales, w1, w2_words, w2_scales, taps, offs, out):
+    nc = tc.nc
+    with ExitStack() as ctx:
+        keep = ctx.enter_context(tc.tile_pool(name="keep", bufs=1))
+        psum = ctx.enter_context(tc.psum_pool(name="psum", bufs=1))
+
+        offsets = keep.tile([P, S // 16], U16, name="offsets")
+        xw = keep.tile([P, T], U32, name="xw", align_bytes=64)
+        xs = keep.tile([P, T], U8, name="xs", align_bytes=64)
+        w1_raw = keep.tile([P, PACK, H], F32, name="w1_raw", align_bytes=64)
+        w1_bf = keep.tile([P, PACK * H], BF16, name="w1_bf", align_bytes=64)
+        w1_q = keep.tile([P, H], U32, name="w1_q", align_bytes=64)
+        w1_s = keep.tile([P, H], U8, name="w1_s", align_bytes=64)
+        w2_q = keep.tile([P, 2 * N], U8, name="w2_q", align_bytes=64)
+        w2_s = keep.tile([P, N], U8, name="w2_s", align_bytes=64)
+        tap = keep.tile([P, PACK * D], F32, name="tap", align_bytes=64)
+        zero = keep.tile([P, PACK, 2], F32, name="zero", align_bytes=64)
+
+        nc.vector.memset(xs[:].bitcast(I32), 0)
+        nc.vector.memset(zero[:], 0.0)
+        nc.vector.memset(w2_s[:].bitcast(I32), 0)
+
+        w1_v = w1.rearrange("(p j) c -> p j c", j=PACK)
+        nc.sync.dma_start(offsets[:], offs)
+        nc.sync.dma_start(w1_raw[:, 0:2, :], w1_v[:, 0:2, :])
+        for q in range(4):
+            nc.sync.dma_start(xs[32 * q : 32 * q + 4, :].bitcast(I32), x_scales[0, 4 * q : 4 * q + 4, :].bitcast(I32))
+        nc.sync.dma_start(w1_raw[:, 2:4, :], w1_v[:, 2:4, :])
+        nc.sync.dma_start(xw[:].bitcast(I32), x_words[0].rearrange("p c r -> p (c r)").bitcast(I32))
+        nc.sync.dma_start(tap[:], taps.rearrange("(p t) d -> p (t d)", t=PACK))
+        nc.sync.dma_start(w2_q[:].bitcast(I32), w2_words[0].bitcast(I32))
+        for q in range(4):
+            nc.sync.dma_start(w2_s[32 * q : 32 * q + 4, :].bitcast(I32), w2_scales[0, 4 * q : 4 * q + 4, :].bitcast(I32))
+
+        starts = [sum(c[0] for c in CHUNKS[:i]) for i in range(len(CHUNKS))]
+        acc = [keep.tile([P, PACK, c[0] + PAD], F32, name="acc%d" % i, align_bytes=64) for i, c in enumerate(CHUNKS)]
+        nc.scalar.activation(acc[0][:, :, 0:2], zero[:], COPY)
+
+        def gather(window, dtype, widths, name):
+            pieces, j0 = [], 0
+            for i, n in enumerate(widths):
+                g = keep.tile([P, n], dtype, name="%s%d" % (name, i), align_bytes=64)
+                nc.vector.tensor_copy(g[:], window[:].indirect(offsets[:, j0 // 16 : (j0 + n) // 16]))
+                pieces.append((j0, n, g))
+                j0 = j0 + n
+            return pieces
+
+        def piece(pieces, j0, n):
+            return [g[:, j0 - a : j0 - a + n] for a, w, g in pieces if a <= j0 and j0 + n <= a + w][0]
+
+        bytes_g = gather(xs, U8, BYTE_GATHERS, "gs")
+
+        dst = w1_bf[:].rearrange("p (t m j) -> p m j t", t=PACK, j=PACK)
+        src = w1_raw[:].rearrange("p j (m t) -> p m j t", t=PACK)
+        nc.scalar.activation(dst[:, 0:W1_SPLIT], src[:, 0:W1_SPLIT], COPY)
+        if W1_SPLIT < P:
+            nc.vector.tensor_copy(dst[:, W1_SPLIT:P], src[:, W1_SPLIT:P])
+        nc.vector.quantize_mx(out=w1_q[:].bitcast(FP8X4), scales=w1_s[:], in_=w1_bf[:])
+
+        words_g = gather(xw, U32, WORD_GATHERS, "gw")
+
+        hs, cur, zs, zq, ob = {}, {}, {}, {}, {}
+
+        def front(c):
+            n, mode, per_bank = CHUNKS[c]
+            j0 = starts[c]
+            hs[c] = []
+            if mode[0] == "S":
+                cur[c] = keep.tile([P, PACK, n], F32, name="cur%d" % c, align_bytes=64)
+            for b in range(PACK // per_bank):
+                bank = psum.tile([P, BANK], F32, name="h%d_%d" % (c, b), tag="h", bufs=H_BANKS)
+                for u in range(per_bank):
+                    t = b * per_bank + u
+                    h = bank[:, u * n : (u + 1) * n]
+                    hs[c].append(h)
+                    nc.tensor.matmul_mx(h, lhsT=w1_q[:, t * P : (t + 1) * P].bitcast(FP8X4), lhsT_scale=w1_s[:, t * P : (t + 1) * P],
+                                        rhs=piece(words_g, j0, n).bitcast(FP8X4), rhs_scale=piece(bytes_g, j0, n), start=True, stop=True)
+                for u in range(per_bank):
+                    t = b * per_bank + u
+                    nc.scalar.activation(acc[c][:, t, 2 : n + 2], hs[c][t], COPY, scale=tap[:, D * t + 2 : D * t + 3])
+                    if mode[0] == "S":
+                        nc.scalar.activation(cur[c][:, t, :], hs[c][t], COPY, scale=tap[:, D * t : D * t + 1])
+
+        def middle(c):
+            n, mode, per_bank = CHUNKS[c]
+            if mode[0] == "V":
+                cur[c] = keep.tile([P, PACK, n], BF16, name="cur%d" % c, align_bytes=64)
+            for b in range(PACK // per_bank):
+                ts = range(b * per_bank, (b + 1) * per_bank)
+                for t in ts:
+                    nc.vector.scalar_tensor_tensor(acc[c][:, t, 1 : n + 1], hs[c][t], tap[:, D * t + 1 : D * t + 2], acc[c][:, t, 1 : n + 1], MULT, ADD)
+                if mode[0] == "V":
+                    for t in ts:
+                        nc.vector.scalar_tensor_tensor(cur[c][:, t, :], hs[c][t], tap[:, D * t : D * t + 1], acc[c][:, t, 0:n], MULT, ADD)
+
+        def halo(c):
+            n = CHUNKS[c - 1][0]
+            nc.vector.tensor_copy(acc[c][:, :, 0:2], acc[c - 1][:, :, n : n + 2])
+
+        def combine(c):
+            n, mode, per_bank = CHUNKS[c]
+            z = keep.tile([P, n * PACK], BF16, name="z%d" % c, align_bytes=64)
+            zs[c] = z
+            step = G_COLS if mode[1] == "G" else n
+            for a in range(0, n, step):
+                zp = z[:, a * PACK : (a + step) * PACK]
+                if mode[0] == "S":
+                    eng = nc.gpsimd if mode[1] == "G" else nc.vector
+                    eng.tensor_tensor(zp.rearrange("p (c i t) -> p c t i", i=2, t=PACK),
+                                      acc[c][:, :, a : a + step].rearrange("p t (c i) -> p c t i", i=2),
+                                      cur[c][:, :, a : a + step].rearrange("p t (c i) -> p c t i", i=2), ADD)
+                elif mode[1] == "G":
+                    nc.gpsimd.tensor_scalar(zp.rearrange("p (c t) -> p c t", t=PACK), cur[c][:, :, a : a + step].rearrange("p t c -> p c t"), 1.0, 0.0, MULT, ADD)
+                elif mode[1] == "S":
+                    nc.scalar.copy(zp.rearrange("p (c i t) -> p c t i", i=4, t=PACK), cur[c][:, :, a : a + step].rearrange("p t (c i) -> p c t i", i=4))
+                else:
+                    nc.vector.tensor_copy(zp.rearrange("p (c i t) -> p c t i", i=4, t=PACK), cur[c][:, :, a : a + step].rearrange("p t (c i) -> p c t i", i=4))
+
+        def second(c):
+            n = CHUNKS[c][0]
+            codes = keep.tile([P, n], U32, name="zq%d" % c, align_bytes=64)
+            scales = keep.tile([P, n], U8, name="zs%d" % c, align_bytes=64)
+            nc.vector.quantize_mx(out=codes[:].bitcast(FP8X4), scales=scales[:], in_=zs[c][:])
+            per = min(2, BANK // n)
+            ob[c] = []
+            for b in range(2 // per):
+                bank = psum.tile([P, BANK], F32, name="o%d_%d" % (c, b), tag="o", bufs=O_BANKS)
+                for u in range(per):
+                    m = b * per + u
+                    nc.tensor.matmul_mx(bank[:, u * n : (u + 1) * n], lhsT=w2_q[:, 2 * P * m : 2 * P * (m + 1)].bitcast(FP4X4), lhsT_scale=w2_s[:, P * m : P * (m + 1)],
+                                        rhs=codes[:].bitcast(FP8X4), rhs_scale=scales[:], start=True, stop=True)
+                ob[c].append(bank[:, 0 : per * n])
+
+        def store(c):
+            n = CHUNKS[c][0]
+            j0 = starts[c]
+            res = keep.tile([P, 2 * n], F32, name="res%d" % c, align_bytes=64)
+            w = 2 * n // len(ob[c])
+            for b, bank in enumerate(ob[c]):
+                if c == len(CHUNKS) - 1 and False:
+                    nc.vector.tensor_copy(res[:, b * w : (b + 1) * w], bank)
+                else:
+                    nc.scalar.copy(res[:, b * w : (b + 1) * w], bank)
+            nc.sync.dma_start(out.rearrange("(m p) j -> p m j", p=P)[:, :, j0 : j0 + n], res[:].rearrange("p (m j) -> p m j", m=2))
+
+        last = len(CHUNKS) - 1
+        front(0)
+        for c in range(last + 1):
+            if c < last:
+                front(c + 1)
+            middle(c)
+            if c > 0:
+                second(c - 1)
+            if c < last:
+                halo(c + 1)
+            combine(c)
+            if c > 0:
+                store(c - 1)
+        second(last)
+        store(last)

@@ -15,19 +15,24 @@ ADD = mybir.AluOpType.add
 COPY = mybir.ActivationFunctionType.Copy
 
 K, T, S, D, H, N = 512, 2048, 1024, 3, 512, 256
-P = 128
-PACK = 4
-BANK = 512
-PAD = 8
 FLOPS = 2 * K * H * S + 2 * H * N * S
 
-CHUNKS = [(256,"SV",2),(256,"SV",2),(256,"SV",2),(256,"SV",2)]
-WORD_GATHERS = [256,256,512]
-BYTE_GATHERS = [1024]
-W1_SPLIT = 80
-G_COLS = 64
+P = 128
+SLOTS = 4
+BANK = 512
+QUADRANT = 32
+CARRY = D - 1
+ROW_PAD = 8
+ALIGN = 64
+
+HEAD = (0, 256)
+BODY = (256, 512)
+TAIL = (768, 256)
+SUMMED = {HEAD: 0, BODY: 256, TAIL: 256}
+PIECE = {HEAD: 256, BODY: 256, TAIL: 128}
 H_BANKS = 6
-O_BANKS = 2
+OUT_BANKS = 2
+W1_SHARE = 64
 
 
 def tile_picked_dconv_none_p_kernel(tc, x_words, x_scales, w1, w2_words, w2_scales, taps, offs, out):
@@ -37,156 +42,180 @@ def tile_picked_dconv_none_p_kernel(tc, x_words, x_scales, w1, w2_words, w2_scal
         psum = ctx.enter_context(tc.psum_pool(name="psum", bufs=1))
 
         offsets = keep.tile([P, S // 16], U16, name="offsets")
-        xw = keep.tile([P, T], U32, name="xw", align_bytes=64)
-        xs = keep.tile([P, T], U8, name="xs", align_bytes=64)
-        w1_raw = keep.tile([P, PACK, H], F32, name="w1_raw", align_bytes=64)
-        w1_bf = keep.tile([P, PACK * H], BF16, name="w1_bf", align_bytes=64)
-        w1_q = keep.tile([P, H], U32, name="w1_q", align_bytes=64)
-        w1_s = keep.tile([P, H], U8, name="w1_s", align_bytes=64)
-        w2_q = keep.tile([P, 2 * N], U8, name="w2_q", align_bytes=64)
-        w2_s = keep.tile([P, N], U8, name="w2_s", align_bytes=64)
-        tap = keep.tile([P, PACK * D], F32, name="tap", align_bytes=64)
-        zero = keep.tile([P, PACK, 2], F32, name="zero", align_bytes=64)
+        x_word_table = keep.tile([P, T], U32, name="x_word_table", align_bytes=ALIGN)
+        x_scale_table = keep.tile([P, T], U8, name="x_scale_table", align_bytes=ALIGN)
+        w1_raw = keep.tile([P, SLOTS, H], F32, name="w1_raw", align_bytes=ALIGN)
+        w1_bf16 = keep.tile([P, SLOTS * H], BF16, name="w1_bf16", align_bytes=ALIGN)
+        w1_codes = keep.tile([P, H], U32, name="w1_codes", align_bytes=ALIGN)
+        w1_scale = keep.tile([P, H], U8, name="w1_scale", align_bytes=ALIGN)
+        w2_codes = keep.tile([P, 2 * N], U8, name="w2_codes", align_bytes=ALIGN)
+        w2_scale = keep.tile([P, N], U8, name="w2_scale", align_bytes=ALIGN)
+        tap_tile = keep.tile([P, SLOTS * D], F32, name="tap_tile", align_bytes=ALIGN)
+        zeros = keep.tile([P, SLOTS, CARRY], F32, name="zeros", align_bytes=ALIGN)
 
-        nc.vector.memset(xs[:].bitcast(I32), 0)
-        nc.vector.memset(zero[:], 0.0)
-        nc.vector.memset(w2_s[:].bitcast(I32), 0)
+        nc.vector.memset(x_scale_table[:].bitcast(I32), 0)
+        nc.vector.memset(zeros[:], 0.0)
+        nc.vector.memset(w2_scale[:].bitcast(I32), 0)
 
-        w1_v = w1.rearrange("(p j) c -> p j c", j=PACK)
+        def load_scales(tile, rows):
+            for r in range(SLOTS):
+                nc.sync.dma_start(tile[r:P:QUADRANT, :].bitcast(I32), rows[0, r:16:SLOTS, :].bitcast(I32))
+
+        w1_rows = w1.rearrange("(p s) i -> p s i", s=SLOTS)
         nc.sync.dma_start(offsets[:], offs)
-        nc.sync.dma_start(w1_raw[:, 0:2, :], w1_v[:, 0:2, :])
-        for q in range(4):
-            nc.sync.dma_start(xs[32 * q : 32 * q + 4, :].bitcast(I32), x_scales[0, 4 * q : 4 * q + 4, :].bitcast(I32))
-        nc.sync.dma_start(w1_raw[:, 2:4, :], w1_v[:, 2:4, :])
-        nc.sync.dma_start(xw[:].bitcast(I32), x_words[0].rearrange("p c r -> p (c r)").bitcast(I32))
-        nc.sync.dma_start(tap[:], taps.rearrange("(p t) d -> p (t d)", t=PACK))
-        nc.sync.dma_start(w2_q[:].bitcast(I32), w2_words[0].bitcast(I32))
-        for q in range(4):
-            nc.sync.dma_start(w2_s[32 * q : 32 * q + 4, :].bitcast(I32), w2_scales[0, 4 * q : 4 * q + 4, :].bitcast(I32))
+        nc.sync.dma_start(w1_raw[:, 0:2, :], w1_rows[:, 0:2, :])
+        load_scales(x_scale_table, x_scales)
+        nc.sync.dma_start(w1_raw[:, 2:4, :], w1_rows[:, 2:4, :])
+        nc.sync.dma_start(x_word_table[:].bitcast(I32), x_words[0].rearrange("p c r -> p (c r)").bitcast(I32))
+        nc.sync.dma_start(tap_tile[:], taps.rearrange("(p t) d -> p (t d)", t=SLOTS))
+        nc.sync.dma_start(w2_codes[:].bitcast(I32), w2_words[0].bitcast(I32))
+        load_scales(w2_scale, w2_scales)
 
-        starts = [sum(c[0] for c in CHUNKS[:i]) for i in range(len(CHUNKS))]
-        acc = [keep.tile([P, PACK, c[0] + PAD], F32, name="acc%d" % i, align_bytes=64) for i, c in enumerate(CHUNKS)]
-        nc.scalar.activation(acc[0][:, :, 0:2], zero[:], COPY)
+        def tap(t, d):
+            return tap_tile[:, D * t + d : D * t + d + 1]
 
-        def gather(window, dtype, widths, name):
-            pieces, j0 = [], 0
-            for i, n in enumerate(widths):
-                g = keep.tile([P, n], dtype, name="%s%d" % (name, i), align_bytes=64)
-                nc.vector.tensor_copy(g[:], window[:].indirect(offsets[:, j0 // 16 : (j0 + n) // 16]))
-                pieces.append((j0, n, g))
-                j0 = j0 + n
-            return pieces
+        acc = {}
+        for st in (HEAD, BODY, TAIL):
+            acc[st] = keep.tile([P, SLOTS, st[1] + ROW_PAD], F32, name="acc%d" % st[0], align_bytes=ALIGN)
+        nc.scalar.activation(acc[HEAD][:, :, 0:CARRY], zeros[:], COPY)
 
-        def piece(pieces, j0, n):
-            return [g[:, j0 - a : j0 - a + n] for a, w, g in pieces if a <= j0 and j0 + n <= a + w][0]
+        def gather(table, dtype, first, width, name):
+            picked = keep.tile([P, width], dtype, name=name, align_bytes=ALIGN)
+            nc.vector.tensor_copy(picked[:], table[:].indirect(offsets[:, first // 16 : (first + width) // 16]))
+            return picked
 
-        bytes_g = gather(xs, U8, BYTE_GATHERS, "gs")
+        x_scale = gather(x_scale_table, U8, 0, S, "x_scale")
 
-        dst = w1_bf[:].rearrange("p (t m j) -> p m j t", t=PACK, j=PACK)
-        src = w1_raw[:].rearrange("p j (m t) -> p m j t", t=PACK)
-        nc.scalar.activation(dst[:, 0:W1_SPLIT], src[:, 0:W1_SPLIT], COPY)
-        if W1_SPLIT < P:
-            nc.vector.tensor_copy(dst[:, W1_SPLIT:P], src[:, W1_SPLIT:P])
-        nc.vector.quantize_mx(out=w1_q[:].bitcast(FP8X4), scales=w1_s[:], in_=w1_bf[:])
+        dealt = w1_bf16[:].rearrange("p (t m s) -> p m s t", t=SLOTS, s=SLOTS)
+        source = w1_raw[:].rearrange("p s (m t) -> p m s t", t=SLOTS)
+        nc.scalar.activation(dealt[:, :, :, 0:2], source[:, :, :, 0:2], COPY)
+        nc.scalar.activation(dealt[:, 0:W1_SHARE, :, 2:4], source[:, 0:W1_SHARE, :, 2:4], COPY)
+        nc.vector.tensor_copy(dealt[:, W1_SHARE:P, :, 2:4], source[:, W1_SHARE:P, :, 2:4])
+        for half in range(2):
+            cols = slice(2 * P * half, 2 * P * (half + 1))
+            nc.vector.quantize_mx(out=w1_codes[:, cols].bitcast(FP8X4), scales=w1_scale[:, cols],
+                                  in_=w1_bf16[:, 2 * H * half : 2 * H * (half + 1)])
 
-        words_g = gather(xw, U32, WORD_GATHERS, "gw")
+        head_words = gather(x_word_table, U32, HEAD[0], HEAD[1], "head_words")
+        rest_words = gather(x_word_table, U32, BODY[0], S - BODY[0], "rest_words")
+        x_word = {HEAD: head_words[:], BODY: rest_words[:, 0 : BODY[1]], TAIL: rest_words[:, BODY[1] : BODY[1] + TAIL[1]]}
 
-        hs, cur, zs, zq, ob = {}, {}, {}, {}, {}
+        planes = {}
+        for st in (HEAD, BODY):
+            planes[st] = keep.tile([P, SLOTS, st[1] - SUMMED[st]], BF16, name="planes%d" % st[0], align_bytes=ALIGN)
+        h, new, z, product = {}, {}, {}, {}
 
-        def front(c):
-            n, mode, per_bank = CHUNKS[c]
-            j0 = starts[c]
-            hs[c] = []
-            if mode[0] == "S":
-                cur[c] = keep.tile([P, PACK, n], F32, name="cur%d" % c, align_bytes=64)
-            for b in range(PACK // per_bank):
-                bank = psum.tile([P, BANK], F32, name="h%d_%d" % (c, b), tag="h", bufs=H_BANKS)
-                for u in range(per_bank):
-                    t = b * per_bank + u
-                    h = bank[:, u * n : (u + 1) * n]
-                    hs[c].append(h)
-                    nc.tensor.matmul_mx(h, lhsT=w1_q[:, t * P : (t + 1) * P].bitcast(FP8X4), lhsT_scale=w1_s[:, t * P : (t + 1) * P],
-                                        rhs=piece(words_g, j0, n).bitcast(FP8X4), rhs_scale=piece(bytes_g, j0, n), start=True, stop=True)
-                for u in range(per_bank):
-                    t = b * per_bank + u
-                    nc.scalar.activation(acc[c][:, t, 2 : n + 2], hs[c][t], COPY, scale=tap[:, D * t + 2 : D * t + 3])
-                    if mode[0] == "S":
-                        nc.scalar.activation(cur[c][:, t, :], hs[c][t], COPY, scale=tap[:, D * t : D * t + 1])
+        def project(st):
+            first, width = st
+            summed = SUMMED[st]
+            if summed:
+                new[st] = keep.tile([P, SLOTS, summed], F32, name="new%d" % first, align_bytes=ALIGN)
+            for t in range(SLOTS):
+                bank = psum.tile([P, BANK], F32, name="h%d_%d" % (first, t), tag="h", bufs=H_BANKS)
+                h[st, t] = bank[:, 0:width]
+                group = slice(t * P, (t + 1) * P)
+                nc.tensor.matmul_mx(h[st, t], lhsT=w1_codes[:, group].bitcast(FP8X4), lhsT_scale=w1_scale[:, group],
+                                    rhs=x_word[st].bitcast(FP8X4), rhs_scale=x_scale[:, first : first + width], start=True, stop=True)
+                nc.scalar.activation(acc[st][:, t, 2 : width + 2], h[st, t], COPY, scale=tap(t, 2))
+                if summed:
+                    nc.scalar.activation(new[st][:, t, :], h[st, t][:, 0:summed], COPY, scale=tap(t, 0))
 
-        def middle(c):
-            n, mode, per_bank = CHUNKS[c]
-            if mode[0] == "V":
-                cur[c] = keep.tile([P, PACK, n], BF16, name="cur%d" % c, align_bytes=64)
-            for b in range(PACK // per_bank):
-                ts = range(b * per_bank, (b + 1) * per_bank)
-                for t in ts:
-                    nc.vector.scalar_tensor_tensor(acc[c][:, t, 1 : n + 1], hs[c][t], tap[:, D * t + 1 : D * t + 2], acc[c][:, t, 1 : n + 1], MULT, ADD)
-                if mode[0] == "V":
-                    for t in ts:
-                        nc.vector.scalar_tensor_tensor(cur[c][:, t, :], hs[c][t], tap[:, D * t : D * t + 1], acc[c][:, t, 0:n], MULT, ADD)
+        def middle_tap(st, t):
+            middle = acc[st][:, t, 1 : st[1] + 1]
+            nc.vector.scalar_tensor_tensor(middle, h[st, t], tap(t, 1), middle, MULT, ADD)
 
-        def halo(c):
-            n = CHUNKS[c - 1][0]
-            nc.vector.tensor_copy(acc[c][:, :, 0:2], acc[c - 1][:, :, n : n + 2])
+        def newest_tap(st, t):
+            cols = slice(SUMMED[st], st[1])
+            nc.vector.scalar_tensor_tensor(planes[st][:, t, :], h[st, t][:, cols], tap(t, 0), acc[st][:, t, cols], MULT, ADD)
 
-        def combine(c):
-            n, mode, per_bank = CHUNKS[c]
-            z = keep.tile([P, n * PACK], BF16, name="z%d" % c, align_bytes=64)
-            zs[c] = z
-            step = G_COLS if mode[1] == "G" else n
-            for a in range(0, n, step):
-                zp = z[:, a * PACK : (a + step) * PACK]
-                if mode[0] == "S":
-                    eng = nc.gpsimd if mode[1] == "G" else nc.vector
-                    eng.tensor_tensor(zp.rearrange("p (c i t) -> p c t i", i=2, t=PACK),
-                                      acc[c][:, :, a : a + step].rearrange("p t (c i) -> p c t i", i=2),
-                                      cur[c][:, :, a : a + step].rearrange("p t (c i) -> p c t i", i=2), ADD)
-                elif mode[1] == "G":
-                    nc.gpsimd.tensor_scalar(zp.rearrange("p (c t) -> p c t", t=PACK), cur[c][:, :, a : a + step].rearrange("p t c -> p c t"), 1.0, 0.0, MULT, ADD)
-                elif mode[1] == "S":
-                    nc.scalar.copy(zp.rearrange("p (c i t) -> p c t i", i=4, t=PACK), cur[c][:, :, a : a + step].rearrange("p t (c i) -> p c t i", i=4))
-                else:
-                    nc.vector.tensor_copy(zp.rearrange("p (c i t) -> p c t i", i=4, t=PACK), cur[c][:, :, a : a + step].rearrange("p t (c i) -> p c t i", i=4))
+        def carry(st, following):
+            nc.vector.tensor_copy(acc[following][:, :, 0:CARRY], acc[st][:, :, st[1] : st[1] + CARRY])
 
-        def second(c):
-            n = CHUNKS[c][0]
-            codes = keep.tile([P, n], U32, name="zq%d" % c, align_bytes=64)
-            scales = keep.tile([P, n], U8, name="zs%d" % c, align_bytes=64)
-            nc.vector.quantize_mx(out=codes[:].bitcast(FP8X4), scales=scales[:], in_=zs[c][:])
-            per = min(2, BANK // n)
-            ob[c] = []
-            for b in range(2 // per):
-                bank = psum.tile([P, BANK], F32, name="o%d_%d" % (c, b), tag="o", bufs=O_BANKS)
-                for u in range(per):
-                    m = b * per + u
-                    nc.tensor.matmul_mx(bank[:, u * n : (u + 1) * n], lhsT=w2_q[:, 2 * P * m : 2 * P * (m + 1)].bitcast(FP4X4), lhsT_scale=w2_s[:, P * m : P * (m + 1)],
-                                        rhs=codes[:].bitcast(FP8X4), rhs_scale=scales[:], start=True, stop=True)
-                ob[c].append(bank[:, 0 : per * n])
+        def z_tile(st, piece):
+            z[st, piece] = keep.tile([P, PIECE[st] * SLOTS], BF16, name="z%d_%d" % (st[0], piece), align_bytes=ALIGN)
+            return z[st, piece][:]
 
-        def store(c):
-            n = CHUNKS[c][0]
-            j0 = starts[c]
-            res = keep.tile([P, 2 * n], F32, name="res%d" % c, align_bytes=64)
-            w = 2 * n // len(ob[c])
-            for b, bank in enumerate(ob[c]):
-                if c == len(CHUNKS) - 1 and False:
-                    nc.vector.tensor_copy(res[:, b * w : (b + 1) * w], bank)
-                else:
-                    nc.scalar.copy(res[:, b * w : (b + 1) * w], bank)
-            nc.sync.dma_start(out.rearrange("(m p) j -> p m j", p=P)[:, :, j0 : j0 + n], res[:].rearrange("p (m j) -> p m j", m=2))
+        def add_and_interleave(st, piece):
+            cols = slice(piece * PIECE[st], (piece + 1) * PIECE[st])
+            nc.vector.tensor_tensor(z_tile(st, piece).rearrange("p (c e t) -> p c t e", e=2, t=SLOTS),
+                                    acc[st][:, :, cols].rearrange("p t (c e) -> p c t e", e=2),
+                                    new[st][:, :, cols].rearrange("p t (c e) -> p c t e", e=2), ADD)
 
-        last = len(CHUNKS) - 1
-        front(0)
-        for c in range(last + 1):
-            if c < last:
-                front(c + 1)
-            middle(c)
-            if c > 0:
-                second(c - 1)
-            if c < last:
-                halo(c + 1)
-            combine(c)
-            if c > 0:
-                store(c - 1)
-        second(last)
-        store(last)
+        def interleave_on_gpsimd(st, piece):
+            nc.gpsimd.tensor_scalar(z_tile(st, piece).rearrange("p (j t) -> p j t", t=SLOTS),
+                                    planes[st][:].rearrange("p t j -> p j t"), 1.0, 0.0, MULT, ADD)
+
+        def interleave_on_scalar(st, piece):
+            nc.scalar.copy(z_tile(st, piece).rearrange("p (c e t) -> p c t e", e=4, t=SLOTS),
+                           planes[st][:].rearrange("p t (c e) -> p c t e", e=4))
+
+        def quantise(st, piece):
+            name = "%d_%d" % (st[0], piece)
+            codes = keep.tile([P, PIECE[st]], U32, name="z_codes" + name, align_bytes=ALIGN)
+            scale = keep.tile([P, PIECE[st]], U8, name="z_scale" + name, align_bytes=ALIGN)
+            nc.vector.quantize_mx(out=codes[:].bitcast(FP8X4), scales=scale[:], in_=z[st, piece][:])
+            return codes, scale
+
+        def second_product(target, half, codes, scale):
+            nc.tensor.matmul_mx(target, lhsT=w2_codes[:, 2 * P * half : 2 * P * (half + 1)].bitcast(FP4X4),
+                                lhsT_scale=w2_scale[:, P * half : P * (half + 1)],
+                                rhs=codes[:].bitcast(FP8X4), rhs_scale=scale[:], start=True, stop=True)
+
+        def multiply(st, piece):
+            width = PIECE[st]
+            codes, scale = quantise(st, piece)
+            bank = psum.tile([P, BANK], F32, name="out%d_%d" % (st[0], piece), tag="out", bufs=OUT_BANKS)
+            for half in range(2):
+                second_product(bank[:, half * width : (half + 1) * width], half, codes, scale)
+            product[st, piece] = bank[:, 0 : 2 * width]
+
+        def store(st, piece):
+            width = PIECE[st]
+            first = st[0] + piece * width
+            result = keep.tile([P, 2 * width], F32, name="result%d" % first, align_bytes=ALIGN)
+            nc.scalar.copy(result[:], product[st, piece])
+            nc.sync.dma_start(out.rearrange("(half p) j -> p half j", p=P)[:, :, first : first + width],
+                              result[:].rearrange("p (half j) -> p half j", half=2))
+
+        def finish_last(st, piece):
+            width = PIECE[st]
+            first = st[0] + piece * width
+            codes, scale = quantise(st, piece)
+            banks = [psum.tile([P, BANK], F32, name="last%d" % half, tag="h", bufs=H_BANKS) for half in range(2)]
+            for half in range(2):
+                second_product(banks[half][:, 0:width], half, codes, scale)
+            low = keep.tile([P, width], F32, name="last_low", align_bytes=ALIGN)
+            nc.vector.tensor_copy(low[:], banks[0][:, 0:width])
+            nc.sync.dma_start(out[0:P, first : first + width], low[:])
+            high = keep.tile([P, width], F32, name="last_high", align_bytes=ALIGN)
+            nc.scalar.copy(high[:], banks[1][:, 0:width])
+            nc.scalar.dma_start(out[P : 2 * P, first : first + width], high[:])
+
+        project(HEAD)
+        project(BODY)
+        for t in range(SLOTS):
+            middle_tap(HEAD, t)
+        carry(HEAD, BODY)
+        for t in range(SLOTS):
+            newest_tap(HEAD, t)
+        interleave_on_gpsimd(HEAD, 0)
+        project(TAIL)
+        for t in range(SLOTS):
+            middle_tap(BODY, t)
+            newest_tap(BODY, t)
+        multiply(HEAD, 0)
+        carry(BODY, TAIL)
+        add_and_interleave(BODY, 0)
+        interleave_on_scalar(BODY, 1)
+        store(HEAD, 0)
+        multiply(BODY, 0)
+        store(BODY, 0)
+        for t in range(SLOTS):
+            middle_tap(TAIL, t)
+        multiply(BODY, 1)
+        add_and_interleave(TAIL, 0)
+        add_and_interleave(TAIL, 1)
+        store(BODY, 1)
+        multiply(TAIL, 0)
+        store(TAIL, 0)
+        finish_last(TAIL, 1)

from contextlib import ExitStack

import concourse.mybir as mybir

F32 = mybir.dt.float32
BF16 = mybir.dt.bfloat16
I32 = mybir.dt.int32
U32 = mybir.dt.uint32
U16 = mybir.dt.uint16
U8 = mybir.dt.uint8
FP8X4 = mybir.dt.float8_e4m3fn_x4
FP4X4 = mybir.dt.float4_e2m1fn_x4
MULT = mybir.AluOpType.mult
ADD = mybir.AluOpType.add
COPY = mybir.ActivationFunctionType.Copy

K, T, S, D, H, N = 512, 2048, 1024, 3, 512, 256
FLOPS = 2 * K * H * S + 2 * H * N * S

P = 128
SLOTS = 4
BANK = 512
QUADRANT = 32
CARRY = D - 1
ROW_PAD = 8
ALIGN = 64

HEAD = (0, 256)
BODY = (256, 512)
TAIL = (768, 256)
SUMMED = {HEAD: 0, BODY: 256, TAIL: 256}
PIECE = {HEAD: 256, BODY: 256, TAIL: 128}
H_BANKS = 6
OUT_BANKS = 2
W1_SHARE = 64


def tile_picked_dconv_none_p_kernel(tc, x_words, x_scales, w1, w2_words, w2_scales, taps, offs, out):
    nc = tc.nc
    with ExitStack() as ctx:
        keep = ctx.enter_context(tc.tile_pool(name="keep", bufs=1))
        psum = ctx.enter_context(tc.psum_pool(name="psum", bufs=1))

        offsets = keep.tile([P, S // 16], U16, name="offsets")
        x_word_table = keep.tile([P, T], U32, name="x_word_table", align_bytes=ALIGN)
        x_scale_table = keep.tile([P, T], U8, name="x_scale_table", align_bytes=ALIGN)
        w1_raw = keep.tile([P, SLOTS, H], F32, name="w1_raw", align_bytes=ALIGN)
        w1_bf16 = keep.tile([P, SLOTS * H], BF16, name="w1_bf16", align_bytes=ALIGN)
        w1_codes = keep.tile([P, H], U32, name="w1_codes", align_bytes=ALIGN)
        w1_scale = keep.tile([P, H], U8, name="w1_scale", align_bytes=ALIGN)
        w2_codes = keep.tile([P, 2 * N], U8, name="w2_codes", align_bytes=ALIGN)
        w2_scale = keep.tile([P, N], U8, name="w2_scale", align_bytes=ALIGN)
        tap_tile = keep.tile([P, SLOTS * D], F32, name="tap_tile", align_bytes=ALIGN)
        zeros = keep.tile([P, SLOTS, CARRY], F32, name="zeros", align_bytes=ALIGN)

        nc.vector.memset(x_scale_table[:].bitcast(I32), 0)
        nc.vector.memset(zeros[:], 0.0)
        nc.vector.memset(w2_scale[:].bitcast(I32), 0)

        def load_scales(tile, rows):
            for r in range(SLOTS):
                nc.sync.dma_start(tile[r:P:QUADRANT, :].bitcast(I32), rows[0, r:16:SLOTS, :].bitcast(I32))

        w1_rows = w1.rearrange("(p s) i -> p s i", s=SLOTS)
        nc.sync.dma_start(offsets[:], offs)
        nc.sync.dma_start(w1_raw[:, 0:2, :], w1_rows[:, 0:2, :])
        load_scales(x_scale_table, x_scales)
        nc.sync.dma_start(w1_raw[:, 2:4, :], w1_rows[:, 2:4, :])
        nc.sync.dma_start(x_word_table[:].bitcast(I32), x_words[0].rearrange("p c r -> p (c r)").bitcast(I32))
        nc.sync.dma_start(tap_tile[:], taps.rearrange("(p t) d -> p (t d)", t=SLOTS))
        nc.sync.dma_start(w2_codes[:].bitcast(I32), w2_words[0].bitcast(I32))
        load_scales(w2_scale, w2_scales)

        def tap(t, d):
            return tap_tile[:, D * t + d : D * t + d + 1]

        acc = {}
        for st in (HEAD, BODY, TAIL):
            acc[st] = keep.tile([P, SLOTS, st[1] + ROW_PAD], F32, name="acc%d" % st[0], align_bytes=ALIGN)
        nc.scalar.activation(acc[HEAD][:, :, 0:CARRY], zeros[:], COPY)

        def gather(table, dtype, first, width, name):
            picked = keep.tile([P, width], dtype, name=name, align_bytes=ALIGN)
            nc.vector.tensor_copy(picked[:], table[:].indirect(offsets[:, first // 16 : (first + width) // 16]))
            return picked

        x_scale = gather(x_scale_table, U8, 0, S, "x_scale")

        dealt = w1_bf16[:].rearrange("p (t m s) -> p m s t", t=SLOTS, s=SLOTS)
        source = w1_raw[:].rearrange("p s (m t) -> p m s t", t=SLOTS)
        nc.scalar.activation(dealt[:, :, :, 0:2], source[:, :, :, 0:2], COPY)
        nc.scalar.activation(dealt[:, 0:W1_SHARE, :, 2:4], source[:, 0:W1_SHARE, :, 2:4], COPY)
        nc.vector.tensor_copy(dealt[:, W1_SHARE:P, :, 2:4], source[:, W1_SHARE:P, :, 2:4])
        for half in range(2):
            cols = slice(2 * P * half, 2 * P * (half + 1))
            nc.vector.quantize_mx(out=w1_codes[:, cols].bitcast(FP8X4), scales=w1_scale[:, cols],
                                  in_=w1_bf16[:, 2 * H * half : 2 * H * (half + 1)])

        head_words = gather(x_word_table, U32, HEAD[0], HEAD[1], "head_words")
        rest_words = gather(x_word_table, U32, BODY[0], S - BODY[0], "rest_words")
        x_word = {HEAD: head_words[:], BODY: rest_words[:, 0 : BODY[1]], TAIL: rest_words[:, BODY[1] : BODY[1] + TAIL[1]]}

        planes = {}
        for st in (HEAD, BODY):
            planes[st] = keep.tile([P, SLOTS, st[1] - SUMMED[st]], BF16, name="planes%d" % st[0], align_bytes=ALIGN)
        h, new, z, product = {}, {}, {}, {}

        def project(st):
            first, width = st
            summed = SUMMED[st]
            if summed:
                new[st] = keep.tile([P, SLOTS, summed], F32, name="new%d" % first, align_bytes=ALIGN)
            for t in range(SLOTS):
                bank = psum.tile([P, BANK], F32, name="h%d_%d" % (first, t), tag="h", bufs=H_BANKS)
                h[st, t] = bank[:, 0:width]
                group = slice(t * P, (t + 1) * P)
                nc.tensor.matmul_mx(h[st, t], lhsT=w1_codes[:, group].bitcast(FP8X4), lhsT_scale=w1_scale[:, group],
                                    rhs=x_word[st].bitcast(FP8X4), rhs_scale=x_scale[:, first : first + width], start=True, stop=True)
                nc.scalar.activation(acc[st][:, t, 2 : width + 2], h[st, t], COPY, scale=tap(t, 2))
                if summed:
                    nc.scalar.activation(new[st][:, t, :], h[st, t][:, 0:summed], COPY, scale=tap(t, 0))

        def middle_tap(st, t):
            middle = acc[st][:, t, 1 : st[1] + 1]
            nc.vector.scalar_tensor_tensor(middle, h[st, t], tap(t, 1), middle, MULT, ADD)

        def newest_tap(st, t):
            cols = slice(SUMMED[st], st[1])
            nc.vector.scalar_tensor_tensor(planes[st][:, t, :], h[st, t][:, cols], tap(t, 0), acc[st][:, t, cols], MULT, ADD)

        def carry(st, following):
            nc.vector.tensor_copy(acc[following][:, :, 0:CARRY], acc[st][:, :, st[1] : st[1] + CARRY])

        def z_tile(st, piece):
            z[st, piece] = keep.tile([P, PIECE[st] * SLOTS], BF16, name="z%d_%d" % (st[0], piece), align_bytes=ALIGN)
            return z[st, piece][:]

        def add_and_interleave(st, piece):
            cols = slice(piece * PIECE[st], (piece + 1) * PIECE[st])
            nc.vector.tensor_tensor(z_tile(st, piece).rearrange("p (c e t) -> p c t e", e=2, t=SLOTS),
                                    acc[st][:, :, cols].rearrange("p t (c e) -> p c t e", e=2),
                                    new[st][:, :, cols].rearrange("p t (c e) -> p c t e", e=2), ADD)

        def interleave_on_gpsimd(st, piece):
            nc.gpsimd.tensor_scalar(z_tile(st, piece).rearrange("p (j t) -> p j t", t=SLOTS),
                                    planes[st][:].rearrange("p t j -> p j t"), 1.0, 0.0, MULT, ADD)

        def interleave_on_scalar(st, piece):
            nc.scalar.copy(z_tile(st, piece).rearrange("p (c e t) -> p c t e", e=4, t=SLOTS),
                           planes[st][:].rearrange("p t (c e) -> p c t e", e=4))

        def quantise(st, piece):
            name = "%d_%d" % (st[0], piece)
            codes = keep.tile([P, PIECE[st]], U32, name="z_codes" + name, align_bytes=ALIGN)
            scale = keep.tile([P, PIECE[st]], U8, name="z_scale" + name, align_bytes=ALIGN)
            nc.vector.quantize_mx(out=codes[:].bitcast(FP8X4), scales=scale[:], in_=z[st, piece][:])
            return codes, scale

        def second_product(target, half, codes, scale):
            nc.tensor.matmul_mx(target, lhsT=w2_codes[:, 2 * P * half : 2 * P * (half + 1)].bitcast(FP4X4),
                                lhsT_scale=w2_scale[:, P * half : P * (half + 1)],
                                rhs=codes[:].bitcast(FP8X4), rhs_scale=scale[:], start=True, stop=True)

        def multiply(st, piece):
            width = PIECE[st]
            codes, scale = quantise(st, piece)
            bank = psum.tile([P, BANK], F32, name="out%d_%d" % (st[0], piece), tag="out", bufs=OUT_BANKS)
            for half in range(2):
                second_product(bank[:, half * width : (half + 1) * width], half, codes, scale)
            product[st, piece] = bank[:, 0 : 2 * width]

        def store(st, piece):
            width = PIECE[st]
            first = st[0] + piece * width
            result = keep.tile([P, 2 * width], F32, name="result%d" % first, align_bytes=ALIGN)
            nc.scalar.copy(result[:], product[st, piece])
            nc.sync.dma_start(out.rearrange("(half p) j -> p half j", p=P)[:, :, first : first + width],
                              result[:].rearrange("p (half j) -> p half j", half=2))

        def finish_last(st, piece):
            width = PIECE[st]
            first = st[0] + piece * width
            codes, scale = quantise(st, piece)
            banks = [psum.tile([P, BANK], F32, name="last%d" % half, tag="h", bufs=H_BANKS) for half in range(2)]
            for half in range(2):
                second_product(banks[half][:, 0:width], half, codes, scale)
            low = keep.tile([P, width], F32, name="last_low", align_bytes=ALIGN)
            nc.vector.tensor_copy(low[:], banks[0][:, 0:width])
            nc.sync.dma_start(out[0:P, first : first + width], low[:])
            high = keep.tile([P, width], F32, name="last_high", align_bytes=ALIGN)
            nc.scalar.copy(high[:], banks[1][:, 0:width])
            nc.scalar.dma_start(out[P : 2 * P, first : first + width], high[:])

        project(HEAD)
        project(BODY)
        for t in range(SLOTS):
            middle_tap(HEAD, t)
        carry(HEAD, BODY)
        for t in range(SLOTS):
            newest_tap(HEAD, t)
        interleave_on_gpsimd(HEAD, 0)
        project(TAIL)
        for t in range(SLOTS):
            middle_tap(BODY, t)
            newest_tap(BODY, t)
        multiply(HEAD, 0)
        carry(BODY, TAIL)
        add_and_interleave(BODY, 0)
        interleave_on_scalar(BODY, 1)
        store(HEAD, 0)
        multiply(BODY, 0)
        store(BODY, 0)
        for t in range(SLOTS):
            middle_tap(TAIL, t)
        multiply(BODY, 1)
        add_and_interleave(TAIL, 0)
        add_and_interleave(TAIL, 1)
        store(BODY, 1)
        multiply(TAIL, 0)
        store(TAIL, 0)
        finish_last(TAIL, 1)
